import numpy as np
import ml_dtypes


def mxq(x, axis, fmt="e4m3"):
    dtype, down = {"e4m3": (ml_dtypes.float8_e4m3fn, 7), "e5m2": (ml_dtypes.float8_e5m2, 14)}[fmt]
    v = np.moveaxis(np.asarray(x, np.float32).astype(ml_dtypes.bfloat16).astype(np.float64), axis, -1)
    blocks = v.reshape(v.shape[:-1] + (-1, 32))
    amax = np.abs(blocks).max(-1, keepdims=True)
    byte = np.maximum(np.where(amax > 0, np.frexp(amax)[1] - 1 + 127, 0) - down, 1)
    scale = np.exp2(byte - 127.0)
    codes = (blocks / scale).astype(np.float32).astype(dtype).astype(np.float64)
    return np.moveaxis((codes * scale).reshape(v.shape), -1, axis)


WIDE = False


def mx_kscale(k):
    if not WIDE:
        return np.ones(k)
    levels = np.array([10, -10, 5, -5, 0])
    if k % 512:
        return np.exp2(np.random.permutation(np.resize(levels, k // 32))).repeat(32)
    a = np.empty((k // 512, 16))
    for p in range(k // 512):
        a[p, :8] = np.random.permutation(np.resize(levels, 8))
        for g in range(8):
            far = levels[np.abs(levels - a[p, g]) >= 10]
            a[p, g + 8] = far[np.random.randint(len(far))]
    return np.exp2(a.ravel()).repeat(32)


def f64(x):
    return np.asarray(x).astype(np.float64)


def striped(idx):
    return np.tile(idx.reshape(-1, 16).T, (8, 1)).astype(np.uint16)


def unstriped(offs):
    return offs[:16].T.reshape(-1).astype(np.int64)


def pack_weight(w):
    k, n = w.shape
    w = f64(np.asarray(w, np.float32).astype(ml_dtypes.bfloat16)).reshape(k // 32, 32, n)
    amax = np.abs(w).max(1)
    byte = np.clip(np.where(amax > 0, np.frexp(amax)[1] - 1 + 127 - 7, 1), 1, 254)
    scaled = (w * np.exp2(127.0 - byte)[:, None, :]).reshape(k, n).astype(np.float32)
    words = np.ascontiguousarray(scaled.reshape(k // 512, 128, 4, n).transpose(0, 1, 3, 2)).astype(ml_dtypes.float8_e4m3fn).view(np.uint8)
    return words, np.ascontiguousarray(byte.astype(np.uint8).reshape(k // 512, 16, n))


def unpack_weight(words, scales):
    g, p, n, _ = words.shape
    vals = np.ascontiguousarray(words).view(ml_dtypes.float8_e4m3fn).astype(np.float64) * np.repeat(np.exp2(scales.astype(np.float64) - 127.0), 8, axis=1)[..., None]
    return vals.transpose(0, 1, 3, 2).reshape(g * 512, n)


def relu(v):
    return np.maximum(v, 0.0)


K, T, S, N, U = 512, 1024, 512, 256, 512
P = 2 ** 7


def setup_inputs():
    n = np.random.standard_normal
    s = mx_kscale(K)[:, None]
    packed_xT = pack_weight(n((K, T)) * s)
    return {
        "x_words": packed_xT[0],
        "x_scales": packed_xT[1],
        "w1": (n((K, N)) / np.sqrt(K) / s).astype(np.float32),
        "will": (np.tile(np.random.uniform(0.5, 2.0, U), (P, 1))).astype(np.float32),
        "peak": (np.tile(np.random.uniform(0.4, 2.0, U), (P, 1))).astype(np.float32),
        "capa": (np.random.uniform(1.0, 4.0, (N, S))).astype(np.float32),
        "offs": striped(np.random.permutation(T)[:S]),
        "lnk1": striped(np.random.randint(0, S, U)),
        "lnk2": striped(np.random.randint(0, S, U)),
        "lnk3": striped(np.random.randint(0, S, U)),
        "fa": striped(np.random.permutation(U)[:S]),
        "fb": striped(np.random.permutation(U)[:S]),
        "fc": striped(np.random.permutation(U)[:S]),
    }


def reference(x_words, x_scales, w1, will, peak, capa, offs, lnk1, lnk2, lnk3, fa, fb, fc):
    xq = unpack_weight(x_words, x_scales)[:, unstriped(offs)]
    y = mxq(f64(w1), 0, "e4m3").T @ xq
    price = 0.6 * (np.log(np.exp(y) + 1.0))
    path = price[:, unstriped(lnk1)] + price[:, unstriped(lnk2)] + price[:, unstriped(lnk3)]
    rate = np.minimum(f64(will)[:1] / (path + 0.1), f64(peak)[:1])
    return relu(price + 0.2 * (rate[:, unstriped(fa)] + rate[:, unstriped(fb)] + rate[:, unstriped(fc)] - f64(capa)))

@@ -1,0 +1,164 @@
+from contextlib import ExitStack
+
+import concourse.mybir as mybir
+
+K, T, S, N = 512, 1024, 512, 256
+FLOPS = 2 * K * S * N
+
+F32 = mybir.dt.float32
+BF16 = mybir.dt.bfloat16
+I32 = mybir.dt.int32
+U32 = mybir.dt.uint32
+U16 = mybir.dt.uint16
+U8 = mybir.dt.uint8
+FP8X4 = mybir.dt.float8_e4m3fn_x4
+ALU = mybir.AluOpType
+ACT = mybir.ActivationFunctionType
+
+P = 128
+PACK = 4
+HALF = S // 2
+HALVES = (slice(0, HALF), slice(HALF, S))
+LIST_HALVES = (slice(0, HALF // 16), slice(HALF // 16, S // 16))
+LOG_WINDOW = 2048
+EXP_CAP = 2.0 ** 60
+
+
+def tile_picked_ynumdl_dual_p_kernel(
+    tc, x_words, x_scales, w1, will, peak, capa, offs, lnk1, lnk2, lnk3, fa, fb, fc, out
+):
+    nc = tc.nc
+    with ExitStack() as ctx:
+        keep = ctx.enter_context(tc.tile_pool(name="keep", bufs=1))
+        psum = ctx.enter_context(tc.psum_pool(name="psum", bufs=1))
+
+        def sbuf(name, shape, dtype=F32):
+            return keep.tile(shape, dtype, name=name, align_bytes=64)
+
+        def load_list(name, src):
+            t = sbuf(name, [P, S // 16], U16)
+            nc.sync.dma_start(t[:], src)
+            return t
+
+        scale_table = sbuf("scale_table", [P, T], U8)
+        nc.gpsimd.memset(scale_table[:].bitcast(I32), 0)
+        w_raw = sbuf("w_raw", [P, PACK, N])
+        nc.sync.dma_start(w_raw[:], w1.rearrange("(p j) n -> p j n", j=PACK))
+        for q in range(4):
+            nc.sync.dma_start(
+                scale_table[32 * q : 32 * q + 4, :].bitcast(I32), x_scales[0, 4 * q : 4 * q + 4, :].bitcast(I32)
+            )
+        offs_t = load_list("offs_t", offs)
+        word_table = sbuf("word_table", [P, T], U32)
+        nc.sync.dma_start(word_table[:].bitcast(I32), x_words[0].rearrange("p n t -> p (n t)").bitcast(I32))
+        lnk = [load_list("lnk%d_t" % (i + 1), src) for i, src in enumerate((lnk1, lnk2, lnk3))]
+        capa_t = sbuf("capa_t", [P, 2, S])
+        nc.sync.dma_start(capa_t[:], capa.rearrange("(b p) j -> p b j", p=P))
+        peak_t = sbuf("peak_t", [P, S])
+        nc.sync.dma_start(peak_t[:], peak)
+        will_t = sbuf("will_t", [P, S])
+        nc.sync.dma_start(will_t[:], will)
+        flows = [load_list(n, src) for n, src in (("fa_t", fa), ("fb_t", fb), ("fc_t", fc))]
+
+        log_window = sbuf("log_window", [P, LOG_WINDOW])
+        nc.gpsimd.memset(log_window[:, S:], 0.0)
+
+        picked_scales = sbuf("picked_scales", [P, S], U8)
+        nc.vector.tensor_copy(picked_scales[:], scale_table[:].indirect(offs_t[:]))
+
+        w_codes = sbuf("w_codes", [P, N], U32)
+        w_scales = sbuf("w_scales", [P, N], U8)
+        for b in range(2):
+            cols = slice(b * P, (b + 1) * P)
+            grouped = sbuf("w_grouped%d" % b, [P, P, PACK], BF16)
+            src = w_raw[:, :, cols].rearrange("p j n -> p n j")
+            if b == 0:
+                nc.vector.tensor_copy(grouped[:], src)
+            else:
+                nc.scalar.copy(grouped[:], src)
+            nc.vector.quantize_mx(
+                out=w_codes[:, cols].bitcast(FP8X4),
+                scales=w_scales[:, cols],
+                in_=grouped[:].rearrange("p n j -> p (n j)"),
+            )
+
+        exp_y = sbuf("exp_y", [P, 2, S])
+        y = []
+        for h in range(2):
+            picked_words = sbuf("picked_words%d" % h, [P, HALF], U32)
+            nc.vector.tensor_copy(picked_words[:], word_table[:].indirect(offs_t[:, LIST_HALVES[h]]))
+            y_h = psum.tile([P, 2, HALF], F32, name="y%d" % h)
+            for b in range(2):
+                cols = slice(b * P, (b + 1) * P)
+                nc.tensor.matmul_mx(
+                    out=y_h[:, b, :],
+                    lhsT=w_codes[:, cols].bitcast(FP8X4),
+                    lhsT_scale=w_scales[:, cols],
+                    rhs=picked_words[:].bitcast(FP8X4),
+                    rhs_scale=picked_scales[:, HALVES[h]],
+                    start=True,
+                    stop=True,
+                )
+            nc.scalar.activation(exp_y[:, :, HALVES[h]], y_h[:], ACT.Exp)
+            y.append(y_h)
+        capped = sbuf("capped", [P, 2, S])
+        for h in range(2):
+            nc.vector.tensor_scalar(capped[:, :, HALVES[h]], exp_y[:, :, HALVES[h]], EXP_CAP, None, ALU.min)
+
+        capa3 = sbuf("capa3", [P, 2, S])
+        nc.vector.tensor_scalar(capa3[:], capa_t[:], 1.0 / 3.0, None, ALU.mult)
+        peak3 = sbuf("peak3", [P, S])
+        nc.vector.tensor_scalar(peak3[:], peak_t[:], 1.0 / 3.0, None, ALU.mult)
+
+        soft = []
+        for b in range(2):
+            log1p = sbuf("log1p%d" % b, [P, S])
+            soft_b = sbuf("soft%d" % b, [P, S])
+            for h in range(2):
+                nc.scalar.activation(log1p[:, HALVES[h]], capped[:, b, HALVES[h]], ACT.Ln, bias=1.0)
+            for h in range(2):
+                nc.vector.tensor_tensor(soft_b[:, HALVES[h]], y[h][:, b, :], log1p[:, HALVES[h]], ALU.max)
+            soft.append(soft_b)
+
+        nc.scalar.activation(log_window[:, 0:S], soft[0][:], ACT.Ln, bias=1.0 / 6.0)
+        first0 = sbuf("first0", [P, S])
+        nc.scalar.activation(first0[:], log_window[:].indirect(lnk[0][:]), ACT.Exp)
+
+        base = [sbuf("base%d" % b, [P, S]) for b in range(2)]
+        nc.gpsimd.tensor_tensor(base[1][:], soft[1][:], capa3[:, 1, :], ALU.subtract)
+
+        def gather_add(name, window, lists, acc):
+            for i, lst in enumerate(lists):
+                nxt = sbuf("%s%d" % (name, i), [P, S])
+                for h in range(2):
+                    nc.vector.tensor_tensor(
+                        nxt[:, HALVES[h]], window[:].indirect(lst[:, LIST_HALVES[h]]), acc[:, HALVES[h]], ALU.add
+                    )
+                acc = nxt
+            return acc
+
+        first1 = sbuf("first1", [P, S])
+        for h in range(2):
+            nc.vector.tensor_copy(first1[:, HALVES[h]], soft[1][:].indirect(lnk[0][:, LIST_HALVES[h]]))
+        path1 = gather_add("path1_", soft[1], lnk[1:], first1)
+        path0 = gather_add("path0_", soft[0], lnk[1:], first0)
+        nc.vector.tensor_tensor(base[0][:], soft[0][:], capa3[:, 0, :], ALU.subtract)
+
+        for b, path, bias in ((1, path1, 0.3), (0, path0, 0.0)):
+            root = sbuf("root%d" % b, [P, S])
+            recip = sbuf("recip%d" % b, [P, S])
+            wish = sbuf("wish%d" % b, [P, S])
+            rate = sbuf("rate%d" % b, [P, S])
+            for h in range(2):
+                nc.scalar.activation(root[:, HALVES[h]], path[:, HALVES[h]], ACT.Abs_reciprocal_sqrt, bias=bias, scale=1.8)
+            for h in range(2):
+                nc.scalar.activation(recip[:, HALVES[h]], root[:, HALVES[h]], ACT.Square)
+            for h in range(2):
+                nc.vector.tensor_tensor(wish[:, HALVES[h]], recip[:, HALVES[h]], will_t[:, HALVES[h]], ALU.mult)
+            for h in range(2):
+                nc.vector.tensor_tensor(rate[:, HALVES[h]], wish[:, HALVES[h]], peak3[:, HALVES[h]], ALU.min)
+            total = gather_add("total%d_" % b, rate, flows, base[b])
+            for h in range(2):
+                result = sbuf("result%d_%d" % (b, h), [P, HALF])
+                nc.scalar.activation(result[:], total[:, HALVES[h]], ACT.Relu, scale=0.6)
+                nc.sync.dma_start(out[b * P : (b + 1) * P, HALVES[h]], result[:])

@@ -1,6 +1,7 @@
 from contextlib import ExitStack
 
 import concourse.mybir as mybir
+from concourse.masks import make_identity
 
 K, T, S, N = 512, 1024, 512, 256
 FLOPS = 2 * K * S * N
@@ -21,6 +22,8 @@ HALF = S // 2
 HALVES = (slice(0, HALF), slice(HALF, S))
 LIST_HALVES = (slice(0, HALF // 16), slice(HALF // 16, S // 16))
 LOG_WINDOW = 2048
+WIDE = 704
+CHUNKS = S // P
 EXP_CAP = 2.0 ** 60
 
 
@@ -32,8 +35,11 @@ def tile_picked_ynumdl_dual_p_kernel(
         keep = ctx.enter_context(tc.tile_pool(name="keep", bufs=1))
         psum = ctx.enter_context(tc.psum_pool(name="psum", bufs=1))
 
-        def sbuf(name, shape, dtype=F32):
-            return keep.tile(shape, dtype, name=name, align_bytes=64)
+        def sbuf(name, shape, dtype=F32, tag=None):
+            return keep.tile(shape, dtype, name=name, tag=tag or name, align_bytes=64)
+
+        def bank(name, shape, index):
+            return psum.tile(shape, F32, name=name, tag="bank%d" % index)
 
         def load_list(name, src):
             t = sbuf(name, [P, S // 16], U16)
@@ -43,25 +49,46 @@ def tile_picked_ynumdl_dual_p_kernel(
         scale_table = sbuf("scale_table", [P, T], U8)
         nc.gpsimd.memset(scale_table[:].bitcast(I32), 0)
         w_raw = sbuf("w_raw", [P, PACK, N])
-        nc.sync.dma_start(w_raw[:], w1.rearrange("(p j) n -> p j n", j=PACK))
+        w_rows = w1.rearrange("(p j) n -> p j n", j=PACK)
+        nc.sync.dma_start(w_raw[:, 0:2, :], w_rows[:, 0:2, :])
         for q in range(4):
             nc.sync.dma_start(
                 scale_table[32 * q : 32 * q + 4, :].bitcast(I32), x_scales[0, 4 * q : 4 * q + 4, :].bitcast(I32)
             )
         offs_t = load_list("offs_t", offs)
+        nc.sync.dma_start(w_raw[:, 2:4, :], w_rows[:, 2:4, :])
         word_table = sbuf("word_table", [P, T], U32)
         nc.sync.dma_start(word_table[:].bitcast(I32), x_words[0].rearrange("p n t -> p (n t)").bitcast(I32))
-        lnk = [load_list("lnk%d_t" % (i + 1), src) for i, src in enumerate((lnk1, lnk2, lnk3))]
         capa_t = sbuf("capa_t", [P, 2, S])
         nc.sync.dma_start(capa_t[:], capa.rearrange("(b p) j -> p b j", p=P))
         peak_t = sbuf("peak_t", [P, S])
         nc.sync.dma_start(peak_t[:], peak)
+        lnk = [load_list("lnk%d_t" % (i + 1), src) for i, src in enumerate((lnk1, lnk2, lnk3))]
         will_t = sbuf("will_t", [P, S])
         nc.sync.dma_start(will_t[:], will)
         flows = [load_list(n, src) for n, src in (("fa_t", fa), ("fb_t", fb), ("fc_t", fc))]
 
+        will_col = sbuf("will_col", [P, CHUNKS])
+        peak_col = sbuf("peak_col", [P, CHUNKS])
+        with nc.allow_non_contiguous_dma(reason="one value a partition and chunk"):
+            nc.sync.dma_start(will_col[:], will[0].rearrange("(c p) -> p c", p=P))
+            nc.sync.dma_start(peak_col[:], peak[0].rearrange("(c p) -> p c", p=P))
+
+        soft = [sbuf("soft0", [P, WIDE]), sbuf("soft1", [P, S])]
+        rate1 = sbuf("rate1", [P, WIDE])
+        nc.gpsimd.memset(soft[0][:, S:], 0.0)
+        nc.scalar.copy(rate1[:, S:], soft[0][:, S:])
+        ident = sbuf("ident", [P, P])
+        make_identity(nc, ident[:])
         log_window = sbuf("log_window", [P, LOG_WINDOW])
         nc.gpsimd.memset(log_window[:, S:], 0.0)
+
+        def chunk(c):
+            return slice(c * P, (c + 1) * P)
+
+        def add_transposed(banks, src, start, stop):
+            for c in range(CHUNKS):
+                nc.tensor.matmul(banks[c][:], src[:, chunk(c)], ident[:], start=start, stop=stop, is_transpose=True)
 
         picked_scales = sbuf("picked_scales", [P, S], U8)
         nc.vector.tensor_copy(picked_scales[:], scale_table[:].indirect(offs_t[:]))
@@ -69,96 +96,135 @@ def tile_picked_ynumdl_dual_p_kernel(
         w_codes = sbuf("w_codes", [P, N], U32)
         w_scales = sbuf("w_scales", [P, N], U8)
         for b in range(2):
-            cols = slice(b * P, (b + 1) * P)
             grouped = sbuf("w_grouped%d" % b, [P, P, PACK], BF16)
-            src = w_raw[:, :, cols].rearrange("p j n -> p n j")
-            if b == 0:
-                nc.vector.tensor_copy(grouped[:], src)
-            else:
-                nc.scalar.copy(grouped[:], src)
+            nc.scalar.copy(grouped[:], w_raw[:, :, chunk(b)].rearrange("p j n -> p n j"))
             nc.vector.quantize_mx(
-                out=w_codes[:, cols].bitcast(FP8X4),
-                scales=w_scales[:, cols],
+                out=w_codes[:, chunk(b)].bitcast(FP8X4),
+                scales=w_scales[:, chunk(b)],
                 in_=grouped[:].rearrange("p n j -> p (n j)"),
             )
 
         exp_y = sbuf("exp_y", [P, 2, S])
-        y = []
+        y = {}
         for h in range(2):
             picked_words = sbuf("picked_words%d" % h, [P, HALF], U32)
             nc.vector.tensor_copy(picked_words[:], word_table[:].indirect(offs_t[:, LIST_HALVES[h]]))
-            y_h = psum.tile([P, 2, HALF], F32, name="y%d" % h)
             for b in range(2):
-                cols = slice(b * P, (b + 1) * P)
+                y[b, h] = bank("y%d%d" % (b, h), [P, HALF], 2 * h + b)
                 nc.tensor.matmul_mx(
-                    out=y_h[:, b, :],
-                    lhsT=w_codes[:, cols].bitcast(FP8X4),
-                    lhsT_scale=w_scales[:, cols],
+                    out=y[b, h][:],
+                    lhsT=w_codes[:, chunk(b)].bitcast(FP8X4),
+                    lhsT_scale=w_scales[:, chunk(b)],
                     rhs=picked_words[:].bitcast(FP8X4),
                     rhs_scale=picked_scales[:, HALVES[h]],
                     start=True,
                     stop=True,
                 )
-            nc.scalar.activation(exp_y[:, :, HALVES[h]], y_h[:], ACT.Exp)
-            y.append(y_h)
+                nc.scalar.activation(exp_y[:, b, HALVES[h]], y[b, h][:], ACT.Exp)
         capped = sbuf("capped", [P, 2, S])
-        for h in range(2):
-            nc.vector.tensor_scalar(capped[:, :, HALVES[h]], exp_y[:, :, HALVES[h]], EXP_CAP, None, ALU.min)
+        for b in range(2):
+            nc.vector.tensor_scalar(capped[:, b, :], exp_y[:, b, :], EXP_CAP, None, ALU.min)
 
-        capa3 = sbuf("capa3", [P, 2, S])
-        nc.vector.tensor_scalar(capa3[:], capa_t[:], 1.0 / 3.0, None, ALU.mult)
+        less_capa = sbuf("less_capa", [P, 2, S])
+        for b in range(2):
+            nc.gpsimd.tensor_scalar(less_capa[:, b, :], capa_t[:, b, :], -1.0 / 3.0, 0.0, ALU.mult, ALU.add)
         peak3 = sbuf("peak3", [P, S])
-        nc.vector.tensor_scalar(peak3[:], peak_t[:], 1.0 / 3.0, None, ALU.mult)
+        nc.gpsimd.tensor_scalar(peak3[:], peak_t[:], 1.0 / 3.0, 0.0, ALU.mult, ALU.add)
 
-        soft = []
         for b in range(2):
             log1p = sbuf("log1p%d" % b, [P, S])
-            soft_b = sbuf("soft%d" % b, [P, S])
             for h in range(2):
                 nc.scalar.activation(log1p[:, HALVES[h]], capped[:, b, HALVES[h]], ACT.Ln, bias=1.0)
             for h in range(2):
-                nc.vector.tensor_tensor(soft_b[:, HALVES[h]], y[h][:, b, :], log1p[:, HALVES[h]], ALU.max)
-            soft.append(soft_b)
+                nc.vector.tensor_tensor(soft[b][:, HALVES[h]], y[b, h][:], log1p[:, HALVES[h]], ALU.max)
 
-        nc.scalar.activation(log_window[:, 0:S], soft[0][:], ACT.Ln, bias=1.0 / 6.0)
-        first0 = sbuf("first0", [P, S])
-        nc.scalar.activation(first0[:], log_window[:].indirect(lnk[0][:]), ACT.Exp)
+        nc.scalar.activation(log_window[:, 0:S], soft[0][:, 0:S], ACT.Ln, bias=1.0 / 6.0)
+        link0 = [sbuf("link0_0", [P, S])]
+        nc.scalar.activation(link0[0][:], log_window[:].indirect(lnk[0][:]), ACT.Exp)
 
-        base = [sbuf("base%d" % b, [P, S]) for b in range(2)]
-        nc.gpsimd.tensor_tensor(base[1][:], soft[1][:], capa3[:, 1, :], ALU.subtract)
+        base0 = sbuf("base0", [P, S])
+        nc.gpsimd.tensor_tensor(base0[:], soft[0][:, 0:S], less_capa[:, 0, :], ALU.add)
 
-        def gather_add(name, window, lists, acc):
-            for i, lst in enumerate(lists):
-                nxt = sbuf("%s%d" % (name, i), [P, S])
-                for h in range(2):
-                    nc.vector.tensor_tensor(
-                        nxt[:, HALVES[h]], window[:].indirect(lst[:, LIST_HALVES[h]]), acc[:, HALVES[h]], ALU.add
-                    )
-                acc = nxt
-            return acc
+        def gather(name, window, lst, tag=None):
+            picked = sbuf(name, [P, S], tag=tag)
+            nc.vector.tensor_copy(picked[:], window[:].indirect(lst[:]))
+            return picked
 
-        first1 = sbuf("first1", [P, S])
+        def gather_add(name, window, lst, acc):
+            nxt = sbuf(name, [P, S])
+            for h in range(2):
+                nc.vector.tensor_tensor(
+                    nxt[:, HALVES[h]], window[:].indirect(lst[:, LIST_HALVES[h]]), acc[:, HALVES[h]], ALU.add
+                )
+            return nxt
+
+        link0.append(gather("link0_1", soft[0], lnk[1]))
+        path1_a = sbuf("path1_a", [P, S])
         for h in range(2):
-            nc.vector.tensor_copy(first1[:, HALVES[h]], soft[1][:].indirect(lnk[0][:, LIST_HALVES[h]]))
-        path1 = gather_add("path1_", soft[1], lnk[1:], first1)
-        path0 = gather_add("path0_", soft[0], lnk[1:], first0)
-        nc.vector.tensor_tensor(base[0][:], soft[0][:], capa3[:, 0, :], ALU.subtract)
+            nc.vector.tensor_copy(path1_a[:, HALVES[h]], soft[1][:].indirect(lnk[0][:, LIST_HALVES[h]]))
+        path1_b = gather_add("path1_b", soft[1], lnk[1], path1_a)
+        path1 = gather_add("path1", soft[1], lnk[2], path1_b)
+        link0.append(gather("link0_2", soft[0], lnk[2], tag="log_window"))
 
-        for b, path, bias in ((1, path1, 0.3), (0, path0, 0.0)):
-            root = sbuf("root%d" % b, [P, S])
-            recip = sbuf("recip%d" % b, [P, S])
-            wish = sbuf("wish%d" % b, [P, S])
-            rate = sbuf("rate%d" % b, [P, S])
-            for h in range(2):
-                nc.scalar.activation(root[:, HALVES[h]], path[:, HALVES[h]], ACT.Abs_reciprocal_sqrt, bias=bias, scale=1.8)
-            for h in range(2):
-                nc.scalar.activation(recip[:, HALVES[h]], root[:, HALVES[h]], ACT.Square)
-            for h in range(2):
-                nc.vector.tensor_tensor(wish[:, HALVES[h]], recip[:, HALVES[h]], will_t[:, HALVES[h]], ALU.mult)
-            for h in range(2):
-                nc.vector.tensor_tensor(rate[:, HALVES[h]], wish[:, HALVES[h]], peak3[:, HALVES[h]], ALU.min)
-            total = gather_add("total%d_" % b, rate, flows, base[b])
-            for h in range(2):
-                result = sbuf("result%d_%d" % (b, h), [P, HALF])
-                nc.scalar.activation(result[:], total[:, HALVES[h]], ACT.Relu, scale=0.6)
-                nc.sync.dma_start(out[b * P : (b + 1) * P, HALVES[h]], result[:])
+        path0_t = [bank("path0_t%d" % c, [P, P], 4 + c) for c in range(CHUNKS)]
+        add_transposed(path0_t, link0[1], True, False)
+        add_transposed(path0_t, link0[0], False, False)
+        add_transposed(path0_t, link0[2], False, True)
+
+        root1 = sbuf("root1", [P, S])
+        recip1 = sbuf("recip1", [P, S])
+        wish1 = sbuf("wish1", [P, S])
+        for h in range(2):
+            nc.scalar.activation(root1[:, HALVES[h]], path1[:, HALVES[h]], ACT.Abs_reciprocal_sqrt, bias=0.3, scale=1.8)
+        for h in range(2):
+            nc.scalar.activation(recip1[:, HALVES[h]], root1[:, HALVES[h]], ACT.Square)
+        for h in range(2):
+            nc.vector.tensor_tensor(wish1[:, HALVES[h]], recip1[:, HALVES[h]], will_t[:, HALVES[h]], ALU.mult)
+        for h in range(2):
+            nc.vector.tensor_tensor(rate1[:, HALVES[h]], wish1[:, HALVES[h]], peak3[:, HALVES[h]], ALU.min)
+
+        root0_t = sbuf("root0_t", [P, S])
+        recip0_t = sbuf("recip0_t", [P, S])
+        rate0_t = sbuf("rate0_t", [P, S])
+        for c in range(CHUNKS):
+            nc.scalar.activation(root0_t[:, chunk(c)], path0_t[c][:], ACT.Abs_reciprocal_sqrt, scale=0.6)
+        nc.scalar.activation(recip0_t[:], root0_t[:], ACT.Square)
+
+        total1_t = [bank("total1_t%d" % c, [P, P], 4 + c) for c in range(CHUNKS)]
+        add_transposed(total1_t, soft[1], True, False)
+        add_transposed(total1_t, less_capa[:, 1, :], False, False)
+        add_transposed(total1_t, gather("flow1_a", rate1, flows[0]), False, False)
+
+        for c in range(CHUNKS):
+            nc.vector.tensor_scalar(
+                rate0_t[:, chunk(c)], recip0_t[:, chunk(c)], will_col[:, c : c + 1], peak_col[:, c : c + 1], ALU.mult, ALU.min
+            )
+        rate0_back = bank("rate0_back", [P, S], 0)
+        for c in range(CHUNKS):
+            nc.tensor.transpose(rate0_back[:, chunk(c)], rate0_t[:, chunk(c)], ident[:])
+        rate0 = sbuf("rate0", [P, S])
+        nc.scalar.activation(rate0[:], rate0_back[:], ACT.Copy, scale=1.0 / 3.0)
+
+        add_transposed(total1_t, gather("flow1_b", rate1, flows[1]), False, False)
+        add_transposed(total1_t, gather("flow1_c", rate1, flows[2], tag="root0_t"), False, True)
+        result1_t = sbuf("result1_t", [P, S])
+        for c in range(CHUNKS):
+            nc.scalar.activation(result1_t[:, chunk(c)], total1_t[c][:], ACT.Relu, scale=0.6)
+        result1_back = bank("result1_back", [P, S], 1)
+        for c in range(CHUNKS):
+            nc.tensor.transpose(result1_back[:, chunk(c)], result1_t[:, chunk(c)], ident[:])
+        result1 = sbuf("result1", [P, S])
+        nc.scalar.copy(result1[:], result1_back[:])
+        nc.sync.dma_start(out[P : 2 * P, :], result1[:])
+
+        total0 = base0
+        for i in range(2):
+            total0 = gather_add("total0_%d" % i, rate0, flows[i], total0)
+        last = sbuf("total0_2", [P, S])
+        for lo, hi, queue in ((0, 256, nc.sync), (256, 384, nc.sync), (384, 512, nc.scalar)):
+            nc.vector.tensor_tensor(
+                last[:, lo:hi], rate0[:].indirect(flows[2][:, lo // 16 : hi // 16]), total0[:, lo:hi], ALU.add
+            )
+            result0 = sbuf("result0_%d" % lo, [P, hi - lo])
+            nc.scalar.activation(result0[:], last[:, lo:hi], ACT.Relu, scale=0.6)
+            queue.dma_start(out[0:P, lo:hi], result0[:])

@@ -125,11 +125,11 @@ def tile_picked_ynumdl_dual_p_kernel(
         for b in range(2):
             nc.vector.tensor_scalar(capped[:, b, :], exp_y[:, b, :], EXP_CAP, None, ALU.min)
 
-        less_capa = sbuf("less_capa", [P, 2, S])
-        for b in range(2):
-            nc.gpsimd.tensor_scalar(less_capa[:, b, :], capa_t[:, b, :], -1.0 / 3.0, 0.0, ALU.mult, ALU.add)
-        peak3 = sbuf("peak3", [P, S])
-        nc.gpsimd.tensor_scalar(peak3[:], peak_t[:], 1.0 / 3.0, 0.0, ALU.mult, ALU.add)
+        thirds = sbuf("thirds", [P, 3, S], tag="word_table")
+        less_capa = thirds[:, 0:2, :]
+        peak3 = thirds[:, 2, :]
+        nc.vector.tensor_scalar(less_capa, capa_t[:], -1.0 / 3.0, None, ALU.mult)
+        nc.vector.tensor_scalar(peak3, peak_t[:], 1.0 / 3.0, None, ALU.mult)
 
         for b in range(2):
             log1p = sbuf("log1p%d" % b, [P, S])

from contextlib import ExitStack

import concourse.mybir as mybir
from concourse.masks import make_identity

K, T, S, N = 512, 1024, 512, 256
FLOPS = 2 * K * S * N

F32 = mybir.dt.float32
BF16 = mybir.dt.bfloat16
I32 = mybir.dt.int32
U32 = mybir.dt.uint32
U16 = mybir.dt.uint16
U8 = mybir.dt.uint8
FP8X4 = mybir.dt.float8_e4m3fn_x4
ALU = mybir.AluOpType
ACT = mybir.ActivationFunctionType

P = 128
PACK = 4
HALF = S // 2
HALVES = (slice(0, HALF), slice(HALF, S))
LIST_HALVES = (slice(0, HALF // 16), slice(HALF // 16, S // 16))
LOG_WINDOW = 2048
WIDE = 704
CHUNKS = S // P
EXP_CAP = 2.0 ** 60


def tile_picked_ynumdl_dual_p_kernel(
    tc, x_words, x_scales, w1, will, peak, capa, offs, lnk1, lnk2, lnk3, fa, fb, fc, out
):
    nc = tc.nc
    with ExitStack() as ctx:
        keep = ctx.enter_context(tc.tile_pool(name="keep", bufs=1))
        psum = ctx.enter_context(tc.psum_pool(name="psum", bufs=1))

        def sbuf(name, shape, dtype=F32, tag=None):
            return keep.tile(shape, dtype, name=name, tag=tag or name, align_bytes=64)

        def bank(name, shape, index):
            return psum.tile(shape, F32, name=name, tag="bank%d" % index)

        def load_list(name, src):
            t = sbuf(name, [P, S // 16], U16)
            nc.sync.dma_start(t[:], src)
            return t

        scale_table = sbuf("scale_table", [P, T], U8)
        nc.gpsimd.memset(scale_table[:].bitcast(I32), 0)
        w_raw = sbuf("w_raw", [P, PACK, N])
        w_rows = w1.rearrange("(p j) n -> p j n", j=PACK)
        nc.sync.dma_start(w_raw[:, 0:2, :], w_rows[:, 0:2, :])
        for q in range(4):
            nc.sync.dma_start(
                scale_table[32 * q : 32 * q + 4, :].bitcast(I32), x_scales[0, 4 * q : 4 * q + 4, :].bitcast(I32)
            )
        offs_t = load_list("offs_t", offs)
        nc.sync.dma_start(w_raw[:, 2:4, :], w_rows[:, 2:4, :])
        word_table = sbuf("word_table", [P, T], U32)
        nc.sync.dma_start(word_table[:].bitcast(I32), x_words[0].rearrange("p n t -> p (n t)").bitcast(I32))
        capa_t = sbuf("capa_t", [P, 2, S])
        nc.sync.dma_start(capa_t[:], capa.rearrange("(b p) j -> p b j", p=P))
        peak_t = sbuf("peak_t", [P, S])
        nc.sync.dma_start(peak_t[:], peak)
        lnk = [load_list("lnk%d_t" % (i + 1), src) for i, src in enumerate((lnk1, lnk2, lnk3))]
        will_t = sbuf("will_t", [P, S])
        nc.sync.dma_start(will_t[:], will)
        flows = [load_list(n, src) for n, src in (("fa_t", fa), ("fb_t", fb), ("fc_t", fc))]

        will_col = sbuf("will_col", [P, CHUNKS])
        peak_col = sbuf("peak_col", [P, CHUNKS])
        with nc.allow_non_contiguous_dma(reason="one value a partition and chunk"):
            nc.sync.dma_start(will_col[:], will[0].rearrange("(c p) -> p c", p=P))
            nc.sync.dma_start(peak_col[:], peak[0].rearrange("(c p) -> p c", p=P))

        soft = [sbuf("soft0", [P, WIDE]), sbuf("soft1", [P, S])]
        rate1 = sbuf("rate1", [P, WIDE])
        nc.gpsimd.memset(soft[0][:, S:], 0.0)
        nc.scalar.copy(rate1[:, S:], soft[0][:, S:])
        ident = sbuf("ident", [P, P])
        make_identity(nc, ident[:])
        log_window = sbuf("log_window", [P, LOG_WINDOW])
        nc.gpsimd.memset(log_window[:, S:], 0.0)

        def chunk(c):
            return slice(c * P, (c + 1) * P)

        def add_transposed(banks, src, start, stop):
            for c in range(CHUNKS):
                nc.tensor.matmul(banks[c][:], src[:, chunk(c)], ident[:], start=start, stop=stop, is_transpose=True)

        picked_scales = sbuf("picked_scales", [P, S], U8)
        nc.vector.tensor_copy(picked_scales[:], scale_table[:].indirect(offs_t[:]))

        w_codes = sbuf("w_codes", [P, N], U32)
        w_scales = sbuf("w_scales", [P, N], U8)
        for b in range(2):
            grouped = sbuf("w_grouped%d" % b, [P, P, PACK], BF16)
            nc.scalar.copy(grouped[:], w_raw[:, :, chunk(b)].rearrange("p j n -> p n j"))
            nc.vector.quantize_mx(
                out=w_codes[:, chunk(b)].bitcast(FP8X4),
                scales=w_scales[:, chunk(b)],
                in_=grouped[:].rearrange("p n j -> p (n j)"),
            )

        exp_y = sbuf("exp_y", [P, 2, S])
        y = {}
        for h in range(2):
            picked_words = sbuf("picked_words%d" % h, [P, HALF], U32)
            nc.vector.tensor_copy(picked_words[:], word_table[:].indirect(offs_t[:, LIST_HALVES[h]]))
            for b in range(2):
                y[b, h] = bank("y%d%d" % (b, h), [P, HALF], 2 * h + b)
                nc.tensor.matmul_mx(
                    out=y[b, h][:],
                    lhsT=w_codes[:, chunk(b)].bitcast(FP8X4),
                    lhsT_scale=w_scales[:, chunk(b)],
                    rhs=picked_words[:].bitcast(FP8X4),
                    rhs_scale=picked_scales[:, HALVES[h]],
                    start=True,
                    stop=True,
                )
                nc.scalar.activation(exp_y[:, b, HALVES[h]], y[b, h][:], ACT.Exp)
        capped = sbuf("capped", [P, 2, S])
        for b in range(2):
            nc.vector.tensor_scalar(capped[:, b, :], exp_y[:, b, :], EXP_CAP, None, ALU.min)

        thirds = sbuf("thirds", [P, 3, S], tag="word_table")
        less_capa = thirds[:, 0:2, :]
        peak3 = thirds[:, 2, :]
        nc.vector.tensor_scalar(less_capa, capa_t[:], -1.0 / 3.0, None, ALU.mult)
        nc.vector.tensor_scalar(peak3, peak_t[:], 1.0 / 3.0, None, ALU.mult)

        for b in range(2):
            log1p = sbuf("log1p%d" % b, [P, S])
            for h in range(2):
                nc.scalar.activation(log1p[:, HALVES[h]], capped[:, b, HALVES[h]], ACT.Ln, bias=1.0)
            for h in range(2):
                nc.vector.tensor_tensor(soft[b][:, HALVES[h]], y[b, h][:], log1p[:, HALVES[h]], ALU.max)

        nc.scalar.activation(log_window[:, 0:S], soft[0][:, 0:S], ACT.Ln, bias=1.0 / 6.0)
        link0 = [sbuf("link0_0", [P, S])]
        nc.scalar.activation(link0[0][:], log_window[:].indirect(lnk[0][:]), ACT.Exp)

        base0 = sbuf("base0", [P, S])
        nc.gpsimd.tensor_tensor(base0[:], soft[0][:, 0:S], less_capa[:, 0, :], ALU.add)

        def gather(name, window, lst, tag=None):
            picked = sbuf(name, [P, S], tag=tag)
            nc.vector.tensor_copy(picked[:], window[:].indirect(lst[:]))
            return picked

        def gather_add(name, window, lst, acc):
            nxt = sbuf(name, [P, S])
            for h in range(2):
                nc.vector.tensor_tensor(
                    nxt[:, HALVES[h]], window[:].indirect(lst[:, LIST_HALVES[h]]), acc[:, HALVES[h]], ALU.add
                )
            return nxt

        link0.append(gather("link0_1", soft[0], lnk[1]))
        path1_a = sbuf("path1_a", [P, S])
        for h in range(2):
            nc.vector.tensor_copy(path1_a[:, HALVES[h]], soft[1][:].indirect(lnk[0][:, LIST_HALVES[h]]))
        path1_b = gather_add("path1_b", soft[1], lnk[1], path1_a)
        path1 = gather_add("path1", soft[1], lnk[2], path1_b)
        link0.append(gather("link0_2", soft[0], lnk[2], tag="log_window"))

        path0_t = [bank("path0_t%d" % c, [P, P], 4 + c) for c in range(CHUNKS)]
        add_transposed(path0_t, link0[1], True, False)
        add_transposed(path0_t, link0[0], False, False)
        add_transposed(path0_t, link0[2], False, True)

        root1 = sbuf("root1", [P, S])
        recip1 = sbuf("recip1", [P, S])
        wish1 = sbuf("wish1", [P, S])
        for h in range(2):
            nc.scalar.activation(root1[:, HALVES[h]], path1[:, HALVES[h]], ACT.Abs_reciprocal_sqrt, bias=0.3, scale=1.8)
        for h in range(2):
            nc.scalar.activation(recip1[:, HALVES[h]], root1[:, HALVES[h]], ACT.Square)
        for h in range(2):
            nc.vector.tensor_tensor(wish1[:, HALVES[h]], recip1[:, HALVES[h]], will_t[:, HALVES[h]], ALU.mult)
        for h in range(2):
            nc.vector.tensor_tensor(rate1[:, HALVES[h]], wish1[:, HALVES[h]], peak3[:, HALVES[h]], ALU.min)

        root0_t = sbuf("root0_t", [P, S])
        recip0_t = sbuf("recip0_t", [P, S])
        rate0_t = sbuf("rate0_t", [P, S])
        for c in range(CHUNKS):
            nc.scalar.activation(root0_t[:, chunk(c)], path0_t[c][:], ACT.Abs_reciprocal_sqrt, scale=0.6)
        nc.scalar.activation(recip0_t[:], root0_t[:], ACT.Square)

        total1_t = [bank("total1_t%d" % c, [P, P], 4 + c) for c in range(CHUNKS)]
        add_transposed(total1_t, soft[1], True, False)
        add_transposed(total1_t, less_capa[:, 1, :], False, False)
        add_transposed(total1_t, gather("flow1_a", rate1, flows[0]), False, False)

        for c in range(CHUNKS):
            nc.vector.tensor_scalar(
                rate0_t[:, chunk(c)], recip0_t[:, chunk(c)], will_col[:, c : c + 1], peak_col[:, c : c + 1], ALU.mult, ALU.min
            )
        rate0_back = bank("rate0_back", [P, S], 0)
        for c in range(CHUNKS):
            nc.tensor.transpose(rate0_back[:, chunk(c)], rate0_t[:, chunk(c)], ident[:])
        rate0 = sbuf("rate0", [P, S])
        nc.scalar.activation(rate0[:], rate0_back[:], ACT.Copy, scale=1.0 / 3.0)

        add_transposed(total1_t, gather("flow1_b", rate1, flows[1]), False, False)
        add_transposed(total1_t, gather("flow1_c", rate1, flows[2], tag="root0_t"), False, True)
        result1_t = sbuf("result1_t", [P, S])
        for c in range(CHUNKS):
            nc.scalar.activation(result1_t[:, chunk(c)], total1_t[c][:], ACT.Relu, scale=0.6)
        result1_back = bank("result1_back", [P, S], 1)
        for c in range(CHUNKS):
            nc.tensor.transpose(result1_back[:, chunk(c)], result1_t[:, chunk(c)], ident[:])
        result1 = sbuf("result1", [P, S])
        nc.scalar.copy(result1[:], result1_back[:])
        nc.sync.dma_start(out[P : 2 * P, :], result1[:])

        total0 = base0
        for i in range(2):
            total0 = gather_add("total0_%d" % i, rate0, flows[i], total0)
        last = sbuf("total0_2", [P, S])
        for lo, hi, queue in ((0, 256, nc.sync), (256, 384, nc.sync), (384, 512, nc.scalar)):
            nc.vector.tensor_tensor(
                last[:, lo:hi], rate0[:].indirect(flows[2][:, lo // 16 : hi // 16]), total0[:, lo:hi], ALU.add
            )
            result0 = sbuf("result0_%d" % lo, [P, hi - lo])
            nc.scalar.activation(result0[:], last[:, lo:hi], ACT.Relu, scale=0.6)
            queue.dma_start(out[0:P, lo:hi], result0[:])
